import numpy as np
CORES = [6,7,14,15,22,23,30,31,38,39,46,47,54,55,62,63]
N = 16
def setup_inputs(rng):
    return {"x": rng.standard_normal((N, 128, 256), dtype=np.float32)}
def reference(x):
    s = x.sum(axis=0, dtype=np.float64).astype(x.dtype)
    return {"y": np.broadcast_to(s, (N,) + s.shape)}

@@ -1,0 +1,81 @@
+from concourse.bass import DstId, RemoteDMATransfer
+
+W = 16
+OWNERS = ((6, 7), (2, 3))
+TARGET = {6: 7, 7: 6, 2: 6, 3: 7}
+
+SCRATCH = {
+    "xs": ("dram", [16, 128, W], "float32"),
+    "pre": ("dram", [4, 128, W], "float32"),
+    "part": ("dram", [10, 128, W], "float32"),
+    "res": ("dram", [16, 128, W], "float32"),
+}
+SEMAPHORES = ["ld", "a1", "a2", "a3", "sent", "st"]
+
+
+def sender(c, d):
+    k = ((d >> 1) - (c >> 1)) % 4
+    if (c & 1) != (d & 1):
+        return (6, 7, 2, 3)[k]
+    return (None, 4, 5, 0)[k]
+
+
+def rank_program(g, core, T, topo):
+    c, me = topo.chip(core), core % 8
+    if me == 1:
+        return
+    is_rank = T.rank_of(core) is not None
+    ri = me - 6
+    sent = [0]
+
+    def did(dst):
+        a = topo.addr(dst)
+        return DstId(rid=a[0], pnc=a[1])
+
+    def tr(srcs, dsts, mask, sem):
+        sent[0] += bin(mask).count("1")
+        return RemoteDMATransfer(dst_ids=[did(x[0]) for x in dsts], dma_engine_mask=mask, remote_sem=sem,
+                                 srcs=srcs, dsts=[x[1] for x in dsts], alu_op=1 if len(srcs) > 1 else 0)
+
+    served = [d for d in range(8) if d != c and sender(c, d) == me]
+
+    if is_rank:
+        g.sync.dma_start(T.xs[:], T.x[:]).then_inc(T.sem.ld, 16)
+        g.wait_ge(T.sem.ld, 16)
+        out = []
+        for d in range(8):
+            if d != c and sender(c, d) != me:
+                for j in range(2):
+                    out.append((T.xs[2 * d + j], 8 * c + sender(c, d), T.pre[2 * ri + j], T.sem.a1))
+        for j in range(2):
+            for o in OWNERS[j]:
+                if o != me:
+                    out.append((T.xs[2 * c + j], 8 * c + o, T.part[8 + ri], T.sem.a2))
+        g.remote_dma_fused([tr([s], [(dc, ap)], 1 << e, sem) for e, (s, dc, ap, sem) in enumerate(out)],
+                           local_sem=T.sem.sent)
+
+    if served:
+        d = served[0]
+        g.wait_ge(T.sem.a1, 2 if is_rank else 4)
+        trs = []
+        for j in range(2):
+            srcs = [T.xs[2 * d + j] if me == 6 + r else T.pre[2 * r + j] for r in range(2)]
+            trs.append(tr(srcs, [(8 * d + o, T.part[c]) for o in OWNERS[j]], 0x0F << (4 * j), T.sem.a2))
+        g.remote_dma_fused(trs, local_sem=T.sem.sent)
+
+    if me in TARGET:
+        j = 0 if is_rank else 1
+        g.wait_ge(T.sem.a2, 7 * 4 + (1 if is_rank else 2))
+        srcs = [T.part[k] for k in range(8) if k != c]
+        srcs += [T.xs[2 * c + j] if me == 6 + r else T.part[8 + r] for r in range(2)]
+        t = TARGET[me]
+        far = [(8 * k + t, T.res[2 * c + j]) for k in range(8) if k != c]
+        g.remote_dma_fused([tr(srcs, far, 0x00FF, T.sem.a3),
+                            tr(srcs, [(8 * c + t, T.res[2 * c + j])], 0xFF00, T.sem.a3)], local_sem=T.sem.sent)
+
+    if is_rank:
+        g.sync.wait_ge(T.sem.a3, 16 * 8)
+        g.sync.dma_start(T.y[:], T.res[:]).then_inc(T.sem.st, 16)
+    g.wait_ge(T.sem.sent, sent[0])
+    if is_rank:
+        g.wait_ge(T.sem.st, 16)

@@ -1,16 +1,17 @@
 from concourse.bass import DstId, RemoteDMATransfer
 
-W = 16
+WS = (16, 16)
 OWNERS = ((6, 7), (2, 3))
 TARGET = {6: 7, 7: 6, 2: 6, 3: 7}
+ROWS = (0, 4 * WS[0], 128)
 
-SCRATCH = {
-    "xs": ("dram", [16, 128, W], "float32"),
-    "pre": ("dram", [4, 128, W], "float32"),
-    "part": ("dram", [10, 128, W], "float32"),
-    "res": ("dram", [16, 128, W], "float32"),
-}
-SEMAPHORES = ["ld", "a1", "a2", "a3", "sent", "st"]
+SCRATCH = {}
+for jj in range(2):
+    SCRATCH["xs%d" % jj] = ("dram", [8, 128, WS[jj]], "float32")
+    SCRATCH["pre%d" % jj] = ("dram", [2, 128, WS[jj]], "float32")
+    SCRATCH["part%d" % jj] = ("dram", [10, 128, WS[jj]], "float32")
+    SCRATCH["res%d" % jj] = ("dram", [8, 128, WS[jj]], "float32")
+SEMAPHORES = ["ld0", "ld1", "a10", "a11", "a2", "a30", "a31", "sent", "st0", "st1"]
 
 
 def sender(c, d):
@@ -27,6 +28,7 @@ def rank_program(g, core, T, topo):
     is_rank = T.rank_of(core) is not None
     ri = me - 6
     sent = [0]
+    queue = (g.sync, g.scalar)
 
     def did(dst):
         a = topo.addr(dst)
@@ -40,42 +42,40 @@ def rank_program(g, core, T, topo):
     served = [d for d in range(8) if d != c and sender(c, d) == me]
 
     if is_rank:
-        g.sync.dma_start(T.xs[:], T.x[:]).then_inc(T.sem.ld, 16)
-        g.wait_ge(T.sem.ld, 16)
-        out = []
-        for d in range(8):
-            if d != c and sender(c, d) != me:
-                for j in range(2):
-                    out.append((T.xs[2 * d + j], 8 * c + sender(c, d), T.pre[2 * ri + j], T.sem.a1))
         for j in range(2):
-            for o in OWNERS[j]:
-                if o != me:
-                    out.append((T.xs[2 * c + j], 8 * c + o, T.part[8 + ri], T.sem.a2))
-        g.remote_dma_fused([tr([s], [(dc, ap)], 1 << e, sem) for e, (s, dc, ap, sem) in enumerate(out)],
-                           local_sem=T.sem.sent)
+            queue[j].dma_start(T["xs%d" % j][:], T.x[ROWS[j]:ROWS[j + 1], :]).then_inc(T.sem["ld%d" % j], 16)
+        for j in range(2):
+            xs = T["xs%d" % j]
+            g.wait_ge(T.sem["ld%d" % j], 16)
+            out = [(xs[d], 8 * c + sender(c, d), T["pre%d" % j][ri], T.sem["a1%d" % j])
+                   for d in range(8) if d != c and sender(c, d) != me]
+            out += [(xs[c], 8 * c + o, T["part%d" % j][8 + ri], T.sem.a2) for o in OWNERS[j] if o != me]
+            g.remote_dma_fused([tr([s], [(dc, ap)], 3 << (2 * e), sem) for e, (s, dc, ap, sem) in enumerate(out)],
+                               local_sem=T.sem.sent)
 
     if served:
         d = served[0]
-        g.wait_ge(T.sem.a1, 2 if is_rank else 4)
-        trs = []
         for j in range(2):
-            srcs = [T.xs[2 * d + j] if me == 6 + r else T.pre[2 * r + j] for r in range(2)]
-            trs.append(tr(srcs, [(8 * d + o, T.part[c]) for o in OWNERS[j]], 0x0F << (4 * j), T.sem.a2))
-        g.remote_dma_fused(trs, local_sem=T.sem.sent)
+            g.wait_ge(T.sem["a1%d" % j], 2 if is_rank else 4)
+            srcs = [T["xs%d" % j][d] if me == 6 + r else T["pre%d" % j][r] for r in range(2)]
+            g.remote_dma_fused([tr(srcs, [(8 * d + o, T["part%d" % j][c]) for o in OWNERS[j]], 0xFF, T.sem.a2)],
+                               local_sem=T.sem.sent)
 
     if me in TARGET:
         j = 0 if is_rank else 1
-        g.wait_ge(T.sem.a2, 7 * 4 + (1 if is_rank else 2))
-        srcs = [T.part[k] for k in range(8) if k != c]
-        srcs += [T.xs[2 * c + j] if me == 6 + r else T.part[8 + r] for r in range(2)]
+        part, res, sem = T["part%d" % j], T["res%d" % j], T.sem["a3%d" % j]
+        g.wait_ge(T.sem.a2, 7 * 8 + (2 if is_rank else 4))
+        srcs = [part[k] for k in range(8) if k != c]
+        srcs += [T["xs%d" % j][c] if me == 6 + r else part[8 + r] for r in range(2)]
         t = TARGET[me]
-        far = [(8 * k + t, T.res[2 * c + j]) for k in range(8) if k != c]
-        g.remote_dma_fused([tr(srcs, far, 0x00FF, T.sem.a3),
-                            tr(srcs, [(8 * c + t, T.res[2 * c + j])], 0xFF00, T.sem.a3)], local_sem=T.sem.sent)
+        g.remote_dma_fused([tr(srcs, [(8 * k + t, res[c]) for k in range(8) if k != c], 0x00FF, sem),
+                            tr(srcs, [(8 * c + t, res[c])], 0xFF00, sem)], local_sem=T.sem.sent)
 
     if is_rank:
-        g.sync.wait_ge(T.sem.a3, 16 * 8)
-        g.sync.dma_start(T.y[:], T.res[:]).then_inc(T.sem.st, 16)
+        for j in range(2):
+            queue[j].wait_ge(T.sem["a3%d" % j], 8 * 8)
+            queue[j].dma_start(T.y[ROWS[j]:ROWS[j + 1], :], T["res%d" % j][:]).then_inc(T.sem["st%d" % j], 16)
     g.wait_ge(T.sem.sent, sent[0])
     if is_rank:
-        g.wait_ge(T.sem.st, 16)
+        g.wait_ge(T.sem.st0, 16)
+        g.wait_ge(T.sem.st1, 16)

@@ -1,16 +1,15 @@
 from concourse.bass import DstId, RemoteDMATransfer
 
-WS = (16, 16)
+W = 16
 OWNERS = ((6, 7), (2, 3))
 TARGET = {6: 7, 7: 6, 2: 6, 3: 7}
-ROWS = (0, 4 * WS[0], 128)
 
 SCRATCH = {}
 for jj in range(2):
-    SCRATCH["xs%d" % jj] = ("dram", [8, 128, WS[jj]], "float32")
-    SCRATCH["pre%d" % jj] = ("dram", [2, 128, WS[jj]], "float32")
-    SCRATCH["part%d" % jj] = ("dram", [10, 128, WS[jj]], "float32")
-    SCRATCH["res%d" % jj] = ("dram", [8, 128, WS[jj]], "float32")
+    SCRATCH["xs%d" % jj] = ("dram", [8, 128, W], "float32")
+    SCRATCH["pre%d" % jj] = ("dram", [2, 128, W], "float32")
+    SCRATCH["part%d" % jj] = ("dram", [10, 128, W], "float32")
+    SCRATCH["res%d" % jj] = ("dram", [8, 128, W], "float32")
 SEMAPHORES = ["ld0", "ld1", "a10", "a11", "a2", "a30", "a31", "sent", "st0", "st1"]
 
 
@@ -29,6 +28,8 @@ def rank_program(g, core, T, topo):
     ri = me - 6
     sent = [0]
     queue = (g.sync, g.scalar)
+    others = sorted([k for k in range(8) if k != c],
+                    key=lambda k: 2 if topo.mates(c, k) else 1 if topo.same_plane(c, k) else 0)
 
     def did(dst):
         a = topo.addr(dst)
@@ -39,42 +40,43 @@ def rank_program(g, core, T, topo):
         return RemoteDMATransfer(dst_ids=[did(x[0]) for x in dsts], dma_engine_mask=mask, remote_sem=sem,
                                  srcs=srcs, dsts=[x[1] for x in dsts], alu_op=1 if len(srcs) > 1 else 0)
 
-    served = [d for d in range(8) if d != c and sender(c, d) == me]
+    def fused(trs):
+        g.remote_dma_fused(trs, local_sem=T.sem.sent)
 
     if is_rank:
         for j in range(2):
-            queue[j].dma_start(T["xs%d" % j][:], T.x[ROWS[j]:ROWS[j + 1], :]).then_inc(T.sem["ld%d" % j], 16)
+            queue[j].dma_start(T["xs%d" % j][:], T.x[64 * j:64 * j + 64, :]).then_inc(T.sem["ld%d" % j], 16)
+        handed = [d for d in others if sender(c, d) != me]
         for j in range(2):
-            xs = T["xs%d" % j]
             g.wait_ge(T.sem["ld%d" % j], 16)
-            out = [(xs[d], 8 * c + sender(c, d), T["pre%d" % j][ri], T.sem["a1%d" % j])
-                   for d in range(8) if d != c and sender(c, d) != me]
-            out += [(xs[c], 8 * c + o, T["part%d" % j][8 + ri], T.sem.a2) for o in OWNERS[j] if o != me]
-            g.remote_dma_fused([tr([s], [(dc, ap)], 3 << (2 * e), sem) for e, (s, dc, ap, sem) in enumerate(out)],
-                               local_sem=T.sem.sent)
+            fused([tr([T["xs%d" % j][d]], [(8 * c + sender(c, d), T["pre%d" % j][ri])], 3 << (2 * e), T.sem["a1%d" % j])
+                   for e, d in enumerate(handed)])
+        own = [(j, o) for j in range(2) for o in OWNERS[j] if o != me]
+        fused([tr([T["xs%d" % j][c]], [(8 * c + o, T["part%d" % j][8 + ri])], 0xF << (4 * e), T.sem.a2)
+               for e, (j, o) in enumerate(own)])
 
+    served = [d for d in others if sender(c, d) == me]
     if served:
         d = served[0]
         for j in range(2):
             g.wait_ge(T.sem["a1%d" % j], 2 if is_rank else 4)
             srcs = [T["xs%d" % j][d] if me == 6 + r else T["pre%d" % j][r] for r in range(2)]
-            g.remote_dma_fused([tr(srcs, [(8 * d + o, T["part%d" % j][c]) for o in OWNERS[j]], 0xFF, T.sem.a2)],
-                               local_sem=T.sem.sent)
+            fused([tr(srcs, [(8 * d + o, T["part%d" % j][c]) for o in OWNERS[j]], 0xFF, T.sem.a2)])
 
     if me in TARGET:
         j = 0 if is_rank else 1
         part, res, sem = T["part%d" % j], T["res%d" % j], T.sem["a3%d" % j]
-        g.wait_ge(T.sem.a2, 7 * 8 + (2 if is_rank else 4))
-        srcs = [part[k] for k in range(8) if k != c]
+        g.wait_ge(T.sem.a2, 7 * 8 + (4 if is_rank else 8))
+        srcs = [part[k] for k in others]
         srcs += [T["xs%d" % j][c] if me == 6 + r else part[8 + r] for r in range(2)]
         t = TARGET[me]
-        g.remote_dma_fused([tr(srcs, [(8 * k + t, res[c]) for k in range(8) if k != c], 0x00FF, sem),
-                            tr(srcs, [(8 * c + t, res[c])], 0xFF00, sem)], local_sem=T.sem.sent)
+        fused([tr(srcs, [(8 * k + t, res[c]) for k in others], 0x00FF, sem),
+               tr(srcs, [(8 * c + t, res[c])], 0xFF00, sem)])
 
     if is_rank:
         for j in range(2):
             queue[j].wait_ge(T.sem["a3%d" % j], 8 * 8)
-            queue[j].dma_start(T.y[ROWS[j]:ROWS[j + 1], :], T["res%d" % j][:]).then_inc(T.sem["st%d" % j], 16)
+            queue[j].dma_start(T.y[64 * j:64 * j + 64, :], T["res%d" % j][:]).then_inc(T.sem["st%d" % j], 16)
     g.wait_ge(T.sem.sent, sent[0])
     if is_rank:
         g.wait_ge(T.sem.st0, 16)

from concourse.bass import DstId, RemoteDMATransfer

W = 16
OWNERS = ((6, 7), (2, 3))
TARGET = {6: 7, 7: 6, 2: 6, 3: 7}

SCRATCH = {}
for jj in range(2):
    SCRATCH["xs%d" % jj] = ("dram", [8, 128, W], "float32")
    SCRATCH["pre%d" % jj] = ("dram", [2, 128, W], "float32")
    SCRATCH["part%d" % jj] = ("dram", [10, 128, W], "float32")
    SCRATCH["res%d" % jj] = ("dram", [8, 128, W], "float32")
SEMAPHORES = ["ld0", "ld1", "a10", "a11", "a2", "a30", "a31", "sent", "st0", "st1"]


def sender(c, d):
    k = ((d >> 1) - (c >> 1)) % 4
    if (c & 1) != (d & 1):
        return (6, 7, 2, 3)[k]
    return (None, 4, 5, 0)[k]


def rank_program(g, core, T, topo):
    c, me = topo.chip(core), core % 8
    if me == 1:
        return
    is_rank = T.rank_of(core) is not None
    ri = me - 6
    sent = [0]
    queue = (g.sync, g.scalar)
    others = sorted([k for k in range(8) if k != c],
                    key=lambda k: 2 if topo.mates(c, k) else 1 if topo.same_plane(c, k) else 0)

    def did(dst):
        a = topo.addr(dst)
        return DstId(rid=a[0], pnc=a[1])

    def tr(srcs, dsts, mask, sem):
        sent[0] += bin(mask).count("1")
        return RemoteDMATransfer(dst_ids=[did(x[0]) for x in dsts], dma_engine_mask=mask, remote_sem=sem,
                                 srcs=srcs, dsts=[x[1] for x in dsts], alu_op=1 if len(srcs) > 1 else 0)

    def fused(trs):
        g.remote_dma_fused(trs, local_sem=T.sem.sent)

    if is_rank:
        for j in range(2):
            queue[j].dma_start(T["xs%d" % j][:], T.x[64 * j:64 * j + 64, :]).then_inc(T.sem["ld%d" % j], 16)
        handed = [d for d in others if sender(c, d) != me]
        for j in range(2):
            g.wait_ge(T.sem["ld%d" % j], 16)
            fused([tr([T["xs%d" % j][d]], [(8 * c + sender(c, d), T["pre%d" % j][ri])], 3 << (2 * e), T.sem["a1%d" % j])
                   for e, d in enumerate(handed)])
        own = [(j, o) for j in range(2) for o in OWNERS[j] if o != me]
        fused([tr([T["xs%d" % j][c]], [(8 * c + o, T["part%d" % j][8 + ri])], 0xF << (4 * e), T.sem.a2)
               for e, (j, o) in enumerate(own)])

    served = [d for d in others if sender(c, d) == me]
    if served:
        d = served[0]
        for j in range(2):
            g.wait_ge(T.sem["a1%d" % j], 2 if is_rank else 4)
            srcs = [T["xs%d" % j][d] if me == 6 + r else T["pre%d" % j][r] for r in range(2)]
            fused([tr(srcs, [(8 * d + o, T["part%d" % j][c]) for o in OWNERS[j]], 0xFF, T.sem.a2)])

    if me in TARGET:
        j = 0 if is_rank else 1
        part, res, sem = T["part%d" % j], T["res%d" % j], T.sem["a3%d" % j]
        g.wait_ge(T.sem.a2, 7 * 8 + (4 if is_rank else 8))
        srcs = [part[k] for k in others]
        srcs += [T["xs%d" % j][c] if me == 6 + r else part[8 + r] for r in range(2)]
        t = TARGET[me]
        fused([tr(srcs, [(8 * k + t, res[c]) for k in others], 0x00FF, sem),
               tr(srcs, [(8 * c + t, res[c])], 0xFF00, sem)])

    if is_rank:
        for j in range(2):
            queue[j].wait_ge(T.sem["a3%d" % j], 8 * 8)
            queue[j].dma_start(T.y[64 * j:64 * j + 64, :], T["res%d" % j][:]).then_inc(T.sem["st%d" % j], 16)
    g.wait_ge(T.sem.sent, sent[0])
    if is_rank:
        g.wait_ge(T.sem.st0, 16)
        g.wait_ge(T.sem.st1, 16)
